import numpy as np
CORES = [2,3,6,7,58,59,62,63,114,115,118,119]
N = 12
TK = 256
D = 128 * N
EPS = 0.01
def setup_inputs(rng):
    x = rng.standard_normal((N, 128, TK), dtype=np.float32) * (0.5 + np.abs(rng.standard_normal((1, 1, TK), dtype=np.float32))) + rng.standard_normal((1, 1, TK), dtype=np.float32)
    return {"x": x, "dy": rng.standard_normal((N, 128, TK), dtype=np.float32) + 0.5 * x + rng.standard_normal((1, 1, TK), dtype=np.float32)}
def setup_inputs_big(rng):
    d = setup_inputs(rng)
    for k in ("x", "dy"): d[k] = (d[k].astype(np.float32) * 1024.0).astype(d[k].dtype)
    return d
def setup_inputs_small(rng):
    d = setup_inputs(rng)
    for k in ("x", "dy"): d[k] = (d[k].astype(np.float32) * (1 / 1024.0)).astype(d[k].dtype)
    return d
def setup_inputs_apart(rng):
    d = setup_inputs(rng)
    f = (10.0 ** rng.permutation(np.linspace(-1.5, 1.5, N))).astype(np.float32).reshape(N, 1, 1)
    for k in ("x",): d[k] = (d[k].astype(np.float32) * f).astype(d[k].dtype)
    return d
def setup_inputs_mixed(rng):
    d = setup_inputs(rng)
    f = (10.0 ** rng.uniform(-3, 3, (1, 1, TK))).astype(np.float32); shape = rng.integers(3, size=(1, 1, TK))
    for k in ("x", "dy"):
        x = d[k].astype(np.float32)
        m = x.mean(axis=(0, 1), keepdims=True); level = m + np.sign(x - m) * np.abs(x - m).mean(axis=(0, 1), keepdims=True) * rng.uniform(0.9, 1.1, x.shape).astype(np.float32)
        other = x * np.where(rng.random(x.shape) < 0.5, 0.1, 1.0).astype(np.float32)
        d[k] = (np.where(shape == 1, level, np.where(shape == 2, other, x)) * f).astype(d[k].dtype)
    return d
def setup_inputs_offset(rng):
    d = setup_inputs(rng)
    x = d["x"]; spread = x.std(axis=(0, 1), keepdims=True)
    d["x"] = (x + spread * rng.uniform(16, 48, (1, 1, TK)) * rng.choice([-1.0, 1.0], (1, 1, TK))).astype(np.float32)
    return d
def reference(x, dy):
    X, DY = x.astype(np.float64), dy.astype(np.float64)
    mu = X.sum(axis=(0, 1)) / D
    rs = 1.0 / np.sqrt(((X - mu) ** 2).sum(axis=(0, 1)) / D + EPS)
    n = (X - mu) * rs
    a = DY.sum(axis=(0, 1)) / D; c = (DY * n).sum(axis=(0, 1)) / D
    return {"dx": (rs * (DY - a - n * c)).astype(np.float32)}

@@ -1,0 +1,187 @@
+from concourse.bass import DstId, RemoteDMATransfer
+from concourse.mybir import AluOpType, AxisListType, ActivationFunctionType
+
+N = 12
+EPS = 0.01
+HB = 128
+NS = 4
+
+_PER_HALF = ["ldx", "ldy", "px", "py", "xs", "prod", "st", "arrA", "arrC", "nsm", "sq", "d", "nsy", "sdd", "e",
+             "sp", "dye", "den", "rc", "de", "sde", "kk", "u", "v", "rs", "diag", "po", "ob", "store"]
+SEMAPHORES = ["ms", "cm", "idn", "sent"] + [n + str(h) for h in (0, 1) for n in _PER_HALF]
+
+SCRATCH = {
+    "xin": ("sbuf", [128, 256], "float32"),
+    "dyin": ("sbuf", [128, 256], "float32"),
+    "R": ("sbuf", [128, 132], "float32"),
+    "ident": ("sbuf", [128, 128], "float32"),
+}
+for _h in ("0", "1"):
+    for _n in ("xs", "jq", "prod", "u", "v", "diag", "ob"):
+        SCRATCH[_n + _h] = ("sbuf", [128, HB], "float32")
+    SCRATCH["land" + _h] = ("sbuf", [128, N * NS], "float32")
+    SCRATCH["W" + _h] = ("sbuf", [128, 2 * N], "float32")
+    SCRATCH["W2" + _h] = ("sbuf", [128, N], "float32")
+    for _n in ("ja", "jb", "jc"):
+        SCRATCH[_n + _h] = ("sbuf", [128, N], "float32")
+    SCRATCH["sc" + _h] = ("sbuf", [128, 12], "float32")
+    for _n in ("px", "py", "po"):
+        SCRATCH[_n + _h] = ("psum", [128, 512], "float32")
+
+
+def _bits(mask):
+    return bin(mask).count("1")
+
+
+def rank_program(g, core, T, topo):
+    if T.rank_of(core) is None:
+        return
+    ranks = list(T.cores)
+    A, X, F = AluOpType, AxisListType.X, ActivationFunctionType
+    S = T.sem
+    pe, dve, act, sp = g.tensor, g.vector, g.scalar, g.sync
+
+    def place(c):
+        same = [q for q in ranks if topo.chip(q) == topo.chip(c) and topo.die(q) == topo.die(c)]
+        return (topo.die(c), same.index(c))
+
+    def fellows(c):
+        return [q for q in ranks if topo.chip(q) != topo.chip(c) and place(q) == place(c)]
+
+    def neighbours(c):
+        return [q for q in ranks if topo.chip(q) == topo.chip(c) and q != c]
+
+    far, near = fellows(core), neighbours(core)
+    for q in far + near:
+        assert topo.may_write(core, q)
+    mask_far = topo.mask(core, far[0])
+    for q in far:
+        mask_far &= topo.mask(core, q)
+    mask_near = topo.mask(core, near[0])
+    for q in near:
+        mask_near &= topo.mask(core, q)
+    grp = 1 + len(far)
+    assert grp * (1 + len(near)) == N
+
+    def dst(q):
+        rid, pid, _ = topo.addr(q)
+        return DstId(rid=rid, pnc=pid)
+
+    for h in (0, 1):
+        c0, c1 = h * HB, (h + 1) * HB
+        sp.dma_start(T.xin[:, c0:c1], T.x[:, c0:c1]).then_inc(S["ldx%d" % h], 16)
+        act.dma_start(T.dyin[:, c0:c1], T.dy[:, c0:c1]).then_inc(S["ldy%d" % h], 16)
+
+    dve.memset(T.R[:, 0:HB], -1.0 / 128.0).then_inc(S.ms, 1)
+    dve.memset(T.R[:, HB:HB + 1], 1.0 / (128.0 * N)).then_inc(S.ms, 1)
+    g.wait_ge(S.ms, 2)
+    g.affine_select(T.R[:, 0:HB], T.R[:, 0:HB], [[-1, HB]], A.not_equal, 127.0 / 128.0, 0, 1).then_inc(S.cm, 1)
+    dve.wait_ge(S.cm, 1)
+    dve.tensor_scalar(T.ident[:], T.R[:, 0:HB], 1.0 / 128.0, None, A.add).then_inc(S.idn, 1)
+
+    pe.wait_ge(S.cm, 1)
+    for h in (0, 1):
+        k = str(h)
+        c0, c1 = h * HB, (h + 1) * HB
+        px, py, land = T["px" + k], T["py" + k], T["land" + k]
+        pe.wait_ge(S["ldx" + k], 16)
+        pe.matmul(px[:, 0:HB + 1], T.xin[:, c0:c1], T.R[:, 0:HB + 1], True, True).then_inc(S["px" + k], 1)
+        pe.wait_ge(S["ldy" + k], 16)
+        pe.matmul(py[:, 0:HB + 1], T.dyin[:, c0:c1], T.R[:, 0:HB + 1], True, True).then_inc(S["py" + k], 1)
+        act.wait_ge(S["px" + k], 1)
+        act.activation(T["xs" + k][:], px[:, 0:HB], F.Copy, scale=1.0 / 128.0).then_inc(S["xs" + k], 1)
+        act.activation(T["jq" + k][:], px[:, 0:HB], F.Square, scale=2.0 ** -3.5,
+                       accum_out=land[:, 2:3]).then_inc(S["st" + k], 1)
+        act.activation(land[:, 0:1], px[:, HB:HB + 1], F.Copy).then_inc(S["st" + k], 1)
+        dve.wait_ge(S["py" + k], 1)
+        dve.wait_ge(S["xs" + k], 1)
+        dve.tensor_tensor(T["prod" + k][:], py[:, 0:HB], T["xs" + k][:], A.mult).then_inc(S["prod" + k], 1)
+        dve.tensor_copy(land[:, 1:2], py[:, HB:HB + 1]).then_inc(S["st" + k], 1)
+        dve.wait_ge(S["prod" + k], 1)
+        dve.tensor_reduce(land[:, 3:4], T["prod" + k][:], X, A.add).then_inc(S["st" + k], 1)
+
+    sent = 0
+    for h in (0, 1):
+        k = str(h)
+        land = T["land" + k]
+        g.wait_ge(S["st" + k], 4)
+        dsts = [land[:, NS * (1 + fellows(q).index(core)):NS * (2 + fellows(q).index(core))] for q in far]
+        g.remote_dma_fused([RemoteDMATransfer(dst_ids=[dst(q) for q in far], dma_engine_mask=mask_far,
+                                              remote_sem=S["arrA" + k], srcs=[land[:, 0:NS]], dsts=dsts, alu_op=0)],
+                           local_sem=S.sent)
+        sent += _bits(mask_far)
+    n_a = len(far) * _bits(mask_far)
+    for h in (0, 1):
+        k = str(h)
+        land = T["land" + k]
+        g.wait_ge(S["arrA" + k], n_a)
+        w = NS * grp
+        dsts = [land[:, w * (1 + neighbours(q).index(core)):w * (2 + neighbours(q).index(core))] for q in near]
+        g.remote_dma_fused([RemoteDMATransfer(dst_ids=[dst(q) for q in near], dma_engine_mask=mask_near,
+                                              remote_sem=S["arrC" + k], srcs=[land[:, 0:w]], dsts=dsts, alu_op=0)],
+                           local_sem=S.sent)
+        sent += _bits(mask_near)
+    n_c = len(near) * _bits(mask_near)
+    g.wait_ge(S.sent, sent)
+
+    fN = float(N)
+    for h in (0, 1):
+        k = str(h)
+        px, py, po, land = T["px" + k], T["py" + k], T["po" + k], T["land" + k]
+        W, W2, sc = T["W" + k], T["W2" + k], T["sc" + k]
+        Mv, Yv, Qv, Pv = (land[:, i:N * NS:NS] for i in range(NS))
+        nsm, nsy, sq, sdd, spc, den, rc, sde, kk, rs = (sc[:, i:i + 1] for i in range(10))
+        d, e = W[:, 0:N], W[:, N:2 * N]
+        for q in (dve, act):
+            q.wait_ge(S["st" + k], 4)
+            q.wait_ge(S["arrA" + k], n_a)
+            q.wait_ge(S["arrC" + k], n_c)
+        dve.tensor_reduce(nsm, Mv, X, A.add, negate=True).then_inc(S["nsm" + k], 1)
+        dve.tensor_reduce(sq, Qv, X, A.add).then_inc(S["sq" + k], 1)
+        dve.wait_ge(S["nsm" + k], 1)
+        dve.tensor_scalar(d, Mv, fN, nsm, A.mult, A.add).then_inc(S["d" + k], 1)
+        act.activation(T["ja" + k][:], Yv, F.Copy, scale=-1.0, accum_out=nsy).then_inc(S["nsy" + k], 1)
+        act.wait_ge(S["nsm" + k], 1)
+        act.activation(T["jb" + k][:], Mv, F.Square, bias=nsm, scale=fN, accum_out=sdd).then_inc(S["sdd" + k], 1)
+        act.wait_ge(S["nsy" + k], 1)
+        act.activation(e, Yv, F.Identity, bias=nsy, scale=fN).then_inc(S["e" + k], 1)
+        act.activation(T["jc" + k][:], Pv, F.Copy, accum_out=spc).then_inc(S["sp" + k], 1)
+        act.wait_ge(S["e" + k], 1)
+        act.activation(py[:, 0:HB], py[:, 0:HB], F.Identity, bias=e[:, 0:1]).then_inc(S["dye" + k], 1)
+        dve.wait_ge(S["sq" + k], 1)
+        dve.wait_ge(S["sdd" + k], 1)
+        dve.tensor_scalar(den, sdd, sq, fN * EPS, A.add, A.add).then_inc(S["den" + k], 1)
+        dve.wait_ge(S["den" + k], 1)
+        dve.reciprocal(rc, den).then_inc(S["rc" + k], 1)
+        dve.wait_ge(S["d" + k], 1)
+        dve.wait_ge(S["e" + k], 1)
+        dve.tensor_tensor(W2[:], d, e, A.mult).then_inc(S["de" + k], 1)
+        dve.wait_ge(S["de" + k], 1)
+        dve.tensor_reduce(sde, W2[:], X, A.add).then_inc(S["sde" + k], 1)
+        dve.wait_ge(S["sde" + k], 1)
+        dve.wait_ge(S["sp" + k], 1)
+        dve.wait_ge(S["rc" + k], 1)
+        dve.tensor_scalar(kk, sde, spc, rc, A.add, A.mult).then_inc(S["kk" + k], 1)
+        act.wait_ge(S["rc" + k], 1)
+        act.activation(rs, rc, F.Sqrt, scale=fN).then_inc(S["rs" + k], 1)
+        act.wait_ge(S["rs" + k], 1)
+        act.wait_ge(S.idn, 1)
+        act.activation(T["diag" + k][:], T.ident[:], F.Identity, scale=rs).then_inc(S["diag" + k], 1)
+        dve.wait_ge(S["kk" + k], 1)
+        dve.tensor_scalar(T["u" + k][:], px[:, 0:HB], d[:, 0:1], kk, A.add, A.mult).then_inc(S["u" + k], 1)
+        dve.wait_ge(S["u" + k], 1)
+        dve.wait_ge(S["dye" + k], 1)
+        dve.tensor_tensor(T["v" + k][:], py[:, 0:HB], T["u" + k][:], A.subtract).then_inc(S["v" + k], 1)
+        pe.wait_ge(S["v" + k], 1)
+        pe.wait_ge(S["diag" + k], 1)
+        pe.matmul(po[:, 0:HB], T["v" + k][:], T["diag" + k][:], True, True).then_inc(S["po" + k], 1)
+
+    for h in (0, 1):
+        k = str(h)
+        c0, c1 = h * HB, (h + 1) * HB
+        dve.wait_ge(S["po" + k], 1)
+        dve.tensor_copy(T["ob" + k][:], T["po" + k][:, 0:HB]).then_inc(S["ob" + k], 1)
+        sp.wait_ge(S["ob" + k], 1)
+        sp.dma_start(T.dx[:, c0:c1], T["ob" + k][:]).then_inc(S["store" + k], 16)
+    for h in (0, 1):
+        sp.wait_ge(S["store%d" % h], 16)

@@ -4,9 +4,10 @@ from concourse.mybir import AluOpType, AxisListType, ActivationFunctionType
 N = 12
 EPS = 0.01
 HB = 128
-NS = 4
+SLW = (8, 4)
+COL = ((0, 4, 1, 5), (0, 1, 2, 3))
 
-_PER_HALF = ["ldx", "ldy", "px", "py", "xs", "prod", "st", "arrA", "arrC", "nsm", "sq", "d", "nsy", "sdd", "e",
+_PER_HALF = ["ldx", "ldy", "px", "py", "xs", "prod", "stx", "sty", "arrA", "arrC", "nsm", "sq", "d", "nsy", "sdd", "e",
              "sp", "dye", "den", "rc", "de", "sde", "kk", "u", "v", "rs", "diag", "po", "ob", "store"]
 SEMAPHORES = ["ms", "cm", "idn", "sent"] + [n + str(h) for h in (0, 1) for n in _PER_HALF]
 
@@ -15,11 +16,12 @@ SCRATCH = {
     "dyin": ("sbuf", [128, 256], "float32"),
     "R": ("sbuf", [128, 132], "float32"),
     "ident": ("sbuf", [128, 128], "float32"),
+    "land0": ("sbuf", [128, N * SLW[0]], "float32"),
+    "land1": ("sbuf", [128, N * SLW[1]], "float32"),
 }
 for _h in ("0", "1"):
     for _n in ("xs", "jq", "prod", "u", "v", "diag", "ob"):
         SCRATCH[_n + _h] = ("sbuf", [128, HB], "float32")
-    SCRATCH["land" + _h] = ("sbuf", [128, N * NS], "float32")
     SCRATCH["W" + _h] = ("sbuf", [128, 2 * N], "float32")
     SCRATCH["W2" + _h] = ("sbuf", [128, N], "float32")
     for _n in ("ja", "jb", "jc"):
@@ -60,6 +62,7 @@ def rank_program(g, core, T, topo):
     mask_near = topo.mask(core, near[0])
     for q in near:
         mask_near &= topo.mask(core, q)
+    mask_side = mask_near & ~mask_far
     grp = 1 + len(far)
     assert grp * (1 + len(near)) == N
 
@@ -74,7 +77,9 @@ def rank_program(g, core, T, topo):
 
     dve.memset(T.R[:, 0:HB], -1.0 / 128.0).then_inc(S.ms, 1)
     dve.memset(T.R[:, HB:HB + 1], 1.0 / (128.0 * N)).then_inc(S.ms, 1)
-    g.wait_ge(S.ms, 2)
+    dve.memset(T.land0[:, 2:4], 0.0).then_inc(S.ms, 1)
+    dve.memset(T.land0[:, 6:8], 0.0).then_inc(S.ms, 1)
+    g.wait_ge(S.ms, 4)
     g.affine_select(T.R[:, 0:HB], T.R[:, 0:HB], [[-1, HB]], A.not_equal, 127.0 / 128.0, 0, 1).then_inc(S.cm, 1)
     dve.wait_ge(S.cm, 1)
     dve.tensor_scalar(T.ident[:], T.R[:, 0:HB], 1.0 / 128.0, None, A.add).then_inc(S.idn, 1)
@@ -83,6 +88,7 @@ def rank_program(g, core, T, topo):
     for h in (0, 1):
         k = str(h)
         c0, c1 = h * HB, (h + 1) * HB
+        cM, cY, cQ, cP = COL[h]
         px, py, land = T["px" + k], T["py" + k], T["land" + k]
         pe.wait_ge(S["ldx" + k], 16)
         pe.matmul(px[:, 0:HB + 1], T.xin[:, c0:c1], T.R[:, 0:HB + 1], True, True).then_inc(S["px" + k], 1)
@@ -91,63 +97,81 @@ def rank_program(g, core, T, topo):
         act.wait_ge(S["px" + k], 1)
         act.activation(T["xs" + k][:], px[:, 0:HB], F.Copy, scale=1.0 / 128.0).then_inc(S["xs" + k], 1)
         act.activation(T["jq" + k][:], px[:, 0:HB], F.Square, scale=2.0 ** -3.5,
-                       accum_out=land[:, 2:3]).then_inc(S["st" + k], 1)
-        act.activation(land[:, 0:1], px[:, HB:HB + 1], F.Copy).then_inc(S["st" + k], 1)
+                       accum_out=land[:, cQ:cQ + 1]).then_inc(S["stx" + k], 1)
+        act.activation(land[:, cM:cM + 1], px[:, HB:HB + 1], F.Copy).then_inc(S["stx" + k], 1)
         dve.wait_ge(S["py" + k], 1)
         dve.wait_ge(S["xs" + k], 1)
         dve.tensor_tensor(T["prod" + k][:], py[:, 0:HB], T["xs" + k][:], A.mult).then_inc(S["prod" + k], 1)
-        dve.tensor_copy(land[:, 1:2], py[:, HB:HB + 1]).then_inc(S["st" + k], 1)
         dve.wait_ge(S["prod" + k], 1)
-        dve.tensor_reduce(land[:, 3:4], T["prod" + k][:], X, A.add).then_inc(S["st" + k], 1)
+        dve.tensor_reduce(land[:, cP:cP + 1], T["prod" + k][:], X, A.add).then_inc(S["sty" + k], 1)
+        act.wait_ge(S["prod" + k], 1)
+        act.activation(land[:, cY:cY + 1], py[:, HB:HB + 1], F.Copy).then_inc(S["sty" + k], 1)
 
+    def send(h, dests, mask, lo, hi, sem):
+        land = T["land%d" % h]
+        if dests is far:
+            base = [SLW[h] * (1 + fellows(q).index(core)) for q in dests]
+        else:
+            base = [SLW[h] * grp * (1 + neighbours(q).index(core)) for q in dests]
+        g.remote_dma_fused([RemoteDMATransfer(dst_ids=[dst(q) for q in dests], dma_engine_mask=mask, remote_sem=sem,
+                                              srcs=[land[:, lo:hi]], dsts=[land[:, b + lo:b + hi] for b in base],
+                                              alu_op=0)], local_sem=S.sent)
+        return _bits(mask)
+
+    bf, bn, bs = _bits(mask_far), _bits(mask_near), _bits(mask_side)
     sent = 0
-    for h in (0, 1):
-        k = str(h)
-        land = T["land" + k]
-        g.wait_ge(S["st" + k], 4)
-        dsts = [land[:, NS * (1 + fellows(q).index(core)):NS * (2 + fellows(q).index(core))] for q in far]
-        g.remote_dma_fused([RemoteDMATransfer(dst_ids=[dst(q) for q in far], dma_engine_mask=mask_far,
-                                              remote_sem=S["arrA" + k], srcs=[land[:, 0:NS]], dsts=dsts, alu_op=0)],
-                           local_sem=S.sent)
-        sent += _bits(mask_far)
-    n_a = len(far) * _bits(mask_far)
-    for h in (0, 1):
-        k = str(h)
-        land = T["land" + k]
-        g.wait_ge(S["arrA" + k], n_a)
-        w = NS * grp
-        dsts = [land[:, w * (1 + neighbours(q).index(core)):w * (2 + neighbours(q).index(core))] for q in near]
-        g.remote_dma_fused([RemoteDMATransfer(dst_ids=[dst(q) for q in near], dma_engine_mask=mask_near,
-                                              remote_sem=S["arrC" + k], srcs=[land[:, 0:w]], dsts=dsts, alu_op=0)],
-                           local_sem=S.sent)
-        sent += _bits(mask_near)
-    n_c = len(near) * _bits(mask_near)
+    g.wait_ge(S.stx0, 2)
+    sent += send(0, far, mask_far, 0, 4, S.arrA0)
+    g.wait_ge(S.sty0, 2)
+    sent += send(0, far, mask_far, 4, 8, S.arrA0)
+    sent += send(0, near, mask_side, 0, 4, S.arrC0)
+    g.wait_ge(S.stx1, 2)
+    g.wait_ge(S.sty1, 2)
+    sent += send(1, far, mask_far, 0, 4, S.arrA1)
+    n_a = (2 * len(far) * bf, len(far) * bf)
+    g.wait_ge(S.arrA0, n_a[0])
+    sent += send(0, near, mask_near, 4, grp * SLW[0], S.arrC0)
+    g.wait_ge(S.arrA1, n_a[1])
+    sent += send(1, near, mask_near, 0, grp * SLW[1], S.arrC1)
+    n_c = (len(near) * (bs + bn), len(near) * bn)
     g.wait_ge(S.sent, sent)
 
     fN = float(N)
+
+    def make_diag(k):
+        act.wait_ge(S["rs" + k], 1)
+        act.wait_ge(S.idn, 1)
+        act.activation(T["diag" + k][:], T.ident[:], F.Identity, scale=T["sc" + k][:, 9:10]).then_inc(S["diag" + k], 1)
+
     for h in (0, 1):
         k = str(h)
         px, py, po, land = T["px" + k], T["py" + k], T["po" + k], T["land" + k]
         W, W2, sc = T["W" + k], T["W2" + k], T["sc" + k]
-        Mv, Yv, Qv, Pv = (land[:, i:N * NS:NS] for i in range(NS))
+        Mv, Yv, Qv, Pv = (land[:, i:N * SLW[h]:SLW[h]] for i in COL[h])
         nsm, nsy, sq, sdd, spc, den, rc, sde, kk, rs = (sc[:, i:i + 1] for i in range(10))
         d, e = W[:, 0:N], W[:, N:2 * N]
         for q in (dve, act):
-            q.wait_ge(S["st" + k], 4)
-            q.wait_ge(S["arrA" + k], n_a)
-            q.wait_ge(S["arrC" + k], n_c)
+            q.wait_ge(S["stx" + k], 2)
+            q.wait_ge(S["sty" + k], 2)
+            q.wait_ge(S["arrA" + k], n_a[h])
+            q.wait_ge(S["arrC" + k], n_c[h])
         dve.tensor_reduce(nsm, Mv, X, A.add, negate=True).then_inc(S["nsm" + k], 1)
         dve.tensor_reduce(sq, Qv, X, A.add).then_inc(S["sq" + k], 1)
         dve.wait_ge(S["nsm" + k], 1)
         dve.tensor_scalar(d, Mv, fN, nsm, A.mult, A.add).then_inc(S["d" + k], 1)
-        act.activation(T["ja" + k][:], Yv, F.Copy, scale=-1.0, accum_out=nsy).then_inc(S["nsy" + k], 1)
+        if h == 0:
+            act.activation(T["ja" + k][:], Yv, F.Copy, scale=-1.0, accum_out=nsy).then_inc(S["nsy" + k], 1)
         act.wait_ge(S["nsm" + k], 1)
         act.activation(T["jb" + k][:], Mv, F.Square, bias=nsm, scale=fN, accum_out=sdd).then_inc(S["sdd" + k], 1)
+        if h == 1:
+            act.activation(T["ja" + k][:], Yv, F.Copy, scale=-1.0, accum_out=nsy).then_inc(S["nsy" + k], 1)
         act.wait_ge(S["nsy" + k], 1)
         act.activation(e, Yv, F.Identity, bias=nsy, scale=fN).then_inc(S["e" + k], 1)
         act.activation(T["jc" + k][:], Pv, F.Copy, accum_out=spc).then_inc(S["sp" + k], 1)
         act.wait_ge(S["e" + k], 1)
-        act.activation(py[:, 0:HB], py[:, 0:HB], F.Identity, bias=e[:, 0:1]).then_inc(S["dye" + k], 1)
+        act.activation(py[:, 0:HB], py[:, 0:HB], F.Identity, bias=W[:, N:N + 1]).then_inc(S["dye" + k], 1)
+        if h == 1:
+            make_diag("0")
         dve.wait_ge(S["sq" + k], 1)
         dve.wait_ge(S["sdd" + k], 1)
         dve.tensor_scalar(den, sdd, sq, fN * EPS, A.add, A.add).then_inc(S["den" + k], 1)
@@ -164,17 +188,19 @@ def rank_program(g, core, T, topo):
         dve.tensor_scalar(kk, sde, spc, rc, A.add, A.mult).then_inc(S["kk" + k], 1)
         act.wait_ge(S["rc" + k], 1)
         act.activation(rs, rc, F.Sqrt, scale=fN).then_inc(S["rs" + k], 1)
-        act.wait_ge(S["rs" + k], 1)
-        act.wait_ge(S.idn, 1)
-        act.activation(T["diag" + k][:], T.ident[:], F.Identity, scale=rs).then_inc(S["diag" + k], 1)
+        if h == 1:
+            make_diag("1")
         dve.wait_ge(S["kk" + k], 1)
-        dve.tensor_scalar(T["u" + k][:], px[:, 0:HB], d[:, 0:1], kk, A.add, A.mult).then_inc(S["u" + k], 1)
+        dve.tensor_scalar(T["u" + k][:], px[:, 0:HB], W[:, 0:1], kk, A.add, A.mult).then_inc(S["u" + k], 1)
         dve.wait_ge(S["u" + k], 1)
         dve.wait_ge(S["dye" + k], 1)
         dve.tensor_tensor(T["v" + k][:], py[:, 0:HB], T["u" + k][:], A.subtract).then_inc(S["v" + k], 1)
+
+    for h in (0, 1):
+        k = str(h)
         pe.wait_ge(S["v" + k], 1)
         pe.wait_ge(S["diag" + k], 1)
-        pe.matmul(po[:, 0:HB], T["v" + k][:], T["diag" + k][:], True, True).then_inc(S["po" + k], 1)
+        pe.matmul(T["po" + k][:, 0:HB], T["v" + k][:], T["diag" + k][:], True, True).then_inc(S["po" + k], 1)
 
     for h in (0, 1):
         k = str(h)

@@ -7,15 +7,16 @@ HB = 128
 SLW = (8, 4)
 COL = ((0, 4, 1, 5), (0, 1, 2, 3))
 
-_PER_HALF = ["ldx", "ldy", "px", "py", "xs", "prod", "stx", "sty", "arrA", "arrC", "nsm", "sq", "d", "nsy", "sdd", "e",
-             "sp", "dye", "den", "rc", "de", "sde", "kk", "u", "v", "rs", "diag", "po", "ob", "store"]
-SEMAPHORES = ["ms", "cm", "idn", "sent"] + [n + str(h) for h in (0, 1) for n in _PER_HALF]
+_PER_HALF = ["ldx", "ldy", "px", "py", "xs", "prod", "stx", "sty", "arrA", "arrC", "nsm", "d", "nsy", "dd", "e",
+             "dye", "xd", "den", "rc", "de", "cv", "u", "v", "diag", "po", "ob", "store"]
+SEMAPHORES = ["ms", "cm", "idn", "idN", "sent"] + [n + str(h) for h in (0, 1) for n in _PER_HALF]
 
 SCRATCH = {
     "xin": ("sbuf", [128, 256], "float32"),
     "dyin": ("sbuf", [128, 256], "float32"),
     "R": ("sbuf", [128, 132], "float32"),
     "ident": ("sbuf", [128, 128], "float32"),
+    "identN": ("sbuf", [128, 128], "float32"),
     "land0": ("sbuf", [128, N * SLW[0]], "float32"),
     "land1": ("sbuf", [128, N * SLW[1]], "float32"),
 }
@@ -24,7 +25,7 @@ for _h in ("0", "1"):
         SCRATCH[_n + _h] = ("sbuf", [128, HB], "float32")
     SCRATCH["W" + _h] = ("sbuf", [128, 2 * N], "float32")
     SCRATCH["W2" + _h] = ("sbuf", [128, N], "float32")
-    for _n in ("ja", "jb", "jc"):
+    for _n in ("ja", "jb", "sa", "sb"):
         SCRATCH[_n + _h] = ("sbuf", [128, N], "float32")
     SCRATCH["sc" + _h] = ("sbuf", [128, 12], "float32")
     for _n in ("px", "py", "po"):
@@ -107,6 +108,9 @@ def rank_program(g, core, T, topo):
         act.wait_ge(S["prod" + k], 1)
         act.activation(land[:, cY:cY + 1], py[:, HB:HB + 1], F.Copy).then_inc(S["sty" + k], 1)
 
+    act.wait_ge(S.idn, 1)
+    act.activation(T.identN[:], T.ident[:], F.Sqrt, scale=float(N * N)).then_inc(S.idN, 1)
+
     def send(h, dests, mask, lo, hi, sem):
         land = T["land%d" % h]
         if dests is far:
@@ -139,16 +143,17 @@ def rank_program(g, core, T, topo):
     fN = float(N)
 
     def make_diag(k):
-        act.wait_ge(S["rs" + k], 1)
-        act.wait_ge(S.idn, 1)
-        act.activation(T["diag" + k][:], T.ident[:], F.Identity, scale=T["sc" + k][:, 9:10]).then_inc(S["diag" + k], 1)
+        act.wait_ge(S["rc" + k], 1)
+        act.wait_ge(S.idN, 1)
+        act.activation(T["diag" + k][:], T.identN[:], F.Sqrt, scale=T["sc" + k][:, 2:3]).then_inc(S["diag" + k], 1)
 
     for h in (0, 1):
         k = str(h)
-        px, py, po, land = T["px" + k], T["py" + k], T["po" + k], T["land" + k]
-        W, W2, sc = T["W" + k], T["W2" + k], T["sc" + k]
+        px, py, land = T["px" + k], T["py" + k], T["land" + k]
+        W, W2, sc, sa, sb = T["W" + k], T["W2" + k], T["sc" + k], T["sa" + k], T["sb" + k]
         Mv, Yv, Qv, Pv = (land[:, i:N * SLW[h]:SLW[h]] for i in COL[h])
-        nsm, nsy, sq, sdd, spc, den, rc, sde, kk, rs = (sc[:, i:i + 1] for i in range(10))
+        nsm, nsy, rc = (sc[:, i:i + 1] for i in range(3))
+        den, cv = sa[:, N - 1:N], sb[:, N - 1:N]
         d, e = W[:, 0:N], W[:, N:2 * N]
         for q in (dve, act):
             q.wait_ge(S["stx" + k], 2)
@@ -156,42 +161,35 @@ def rank_program(g, core, T, topo):
             q.wait_ge(S["arrA" + k], n_a[h])
             q.wait_ge(S["arrC" + k], n_c[h])
         dve.tensor_reduce(nsm, Mv, X, A.add, negate=True).then_inc(S["nsm" + k], 1)
-        dve.tensor_reduce(sq, Qv, X, A.add).then_inc(S["sq" + k], 1)
+        act.activation(T["ja" + k][:], Yv, F.Copy, scale=-1.0, accum_out=nsy).then_inc(S["nsy" + k], 1)
         dve.wait_ge(S["nsm" + k], 1)
         dve.tensor_scalar(d, Mv, fN, nsm, A.mult, A.add).then_inc(S["d" + k], 1)
-        if h == 0:
-            act.activation(T["ja" + k][:], Yv, F.Copy, scale=-1.0, accum_out=nsy).then_inc(S["nsy" + k], 1)
         act.wait_ge(S["nsm" + k], 1)
-        act.activation(T["jb" + k][:], Mv, F.Square, bias=nsm, scale=fN, accum_out=sdd).then_inc(S["sdd" + k], 1)
-        if h == 1:
-            act.activation(T["ja" + k][:], Yv, F.Copy, scale=-1.0, accum_out=nsy).then_inc(S["nsy" + k], 1)
+        act.activation(T["jb" + k][:], Mv, F.Square, bias=nsm, scale=fN).then_inc(S["dd" + k], 1)
         act.wait_ge(S["nsy" + k], 1)
         act.activation(e, Yv, F.Identity, bias=nsy, scale=fN).then_inc(S["e" + k], 1)
-        act.activation(T["jc" + k][:], Pv, F.Copy, accum_out=spc).then_inc(S["sp" + k], 1)
         act.wait_ge(S["e" + k], 1)
         act.activation(py[:, 0:HB], py[:, 0:HB], F.Identity, bias=W[:, N:N + 1]).then_inc(S["dye" + k], 1)
+        act.wait_ge(S["d" + k], 1)
+        act.wait_ge(S["xs" + k], 1)
+        act.activation(px[:, 0:HB], px[:, 0:HB], F.Identity, bias=W[:, 0:1]).then_inc(S["xd" + k], 1)
         if h == 1:
             make_diag("0")
-        dve.wait_ge(S["sq" + k], 1)
-        dve.wait_ge(S["sdd" + k], 1)
-        dve.tensor_scalar(den, sdd, sq, fN * EPS, A.add, A.add).then_inc(S["den" + k], 1)
+        dve.wait_ge(S["dd" + k], 1)
+        dve.tensor_tensor_scan(sa[:], Qv, T["jb" + k][:], fN * EPS, A.add, A.add).then_inc(S["den" + k], 1)
         dve.wait_ge(S["den" + k], 1)
         dve.reciprocal(rc, den).then_inc(S["rc" + k], 1)
         dve.wait_ge(S["d" + k], 1)
         dve.wait_ge(S["e" + k], 1)
         dve.tensor_tensor(W2[:], d, e, A.mult).then_inc(S["de" + k], 1)
         dve.wait_ge(S["de" + k], 1)
-        dve.tensor_reduce(sde, W2[:], X, A.add).then_inc(S["sde" + k], 1)
-        dve.wait_ge(S["sde" + k], 1)
-        dve.wait_ge(S["sp" + k], 1)
-        dve.wait_ge(S["rc" + k], 1)
-        dve.tensor_scalar(kk, sde, spc, rc, A.add, A.mult).then_inc(S["kk" + k], 1)
-        act.wait_ge(S["rc" + k], 1)
-        act.activation(rs, rc, F.Sqrt, scale=fN).then_inc(S["rs" + k], 1)
+        dve.tensor_tensor_scan(sb[:], Pv, W2[:], 0.0, A.add, A.add).then_inc(S["cv" + k], 1)
         if h == 1:
             make_diag("1")
-        dve.wait_ge(S["kk" + k], 1)
-        dve.tensor_scalar(T["u" + k][:], px[:, 0:HB], W[:, 0:1], kk, A.add, A.mult).then_inc(S["u" + k], 1)
+        dve.wait_ge(S["cv" + k], 1)
+        dve.wait_ge(S["rc" + k], 1)
+        dve.wait_ge(S["xd" + k], 1)
+        dve.tensor_scalar(T["u" + k][:], px[:, 0:HB], rc, cv, A.mult, A.mult).then_inc(S["u" + k], 1)
         dve.wait_ge(S["u" + k], 1)
         dve.wait_ge(S["dye" + k], 1)
         dve.tensor_tensor(T["v" + k][:], py[:, 0:HB], T["u" + k][:], A.subtract).then_inc(S["v" + k], 1)

@@ -6,6 +6,8 @@ EPS = 0.01
 HB = 128
 SLW = (8, 4)
 COL = ((0, 4, 1, 5), (0, 1, 2, 3))
+STAGES = 8
+LEAD = 4
 
 _PER_HALF = ["ldx", "ldy", "px", "py", "xs", "prod", "stx", "sty", "arrA", "arrC", "nsm", "d", "nsy", "dd", "e",
              "dye", "xd", "den", "rc", "de", "cv", "u", "v", "diag", "po", "ob", "store"]
@@ -142,12 +144,7 @@ def rank_program(g, core, T, topo):
 
     fN = float(N)
 
-    def make_diag(k):
-        act.wait_ge(S["rc" + k], 1)
-        act.wait_ge(S.idN, 1)
-        act.activation(T["diag" + k][:], T.identN[:], F.Sqrt, scale=T["sc" + k][:, 2:3]).then_inc(S["diag" + k], 1)
-
-    for h in (0, 1):
+    def stage(s, h):
         k = str(h)
         px, py, land = T["px" + k], T["py" + k], T["land" + k]
         W, W2, sc, sa, sb = T["W" + k], T["W2" + k], T["sc" + k], T["sa" + k], T["sb" + k]
@@ -155,44 +152,59 @@ def rank_program(g, core, T, topo):
         nsm, nsy, rc = (sc[:, i:i + 1] for i in range(3))
         den, cv = sa[:, N - 1:N], sb[:, N - 1:N]
         d, e = W[:, 0:N], W[:, N:2 * N]
-        for q in (dve, act):
-            q.wait_ge(S["stx" + k], 2)
-            q.wait_ge(S["sty" + k], 2)
-            q.wait_ge(S["arrA" + k], n_a[h])
-            q.wait_ge(S["arrC" + k], n_c[h])
-        dve.tensor_reduce(nsm, Mv, X, A.add, negate=True).then_inc(S["nsm" + k], 1)
-        act.activation(T["ja" + k][:], Yv, F.Copy, scale=-1.0, accum_out=nsy).then_inc(S["nsy" + k], 1)
-        dve.wait_ge(S["nsm" + k], 1)
-        dve.tensor_scalar(d, Mv, fN, nsm, A.mult, A.add).then_inc(S["d" + k], 1)
-        act.wait_ge(S["nsm" + k], 1)
-        act.activation(T["jb" + k][:], Mv, F.Square, bias=nsm, scale=fN).then_inc(S["dd" + k], 1)
-        act.wait_ge(S["nsy" + k], 1)
-        act.activation(e, Yv, F.Identity, bias=nsy, scale=fN).then_inc(S["e" + k], 1)
-        act.wait_ge(S["e" + k], 1)
-        act.activation(py[:, 0:HB], py[:, 0:HB], F.Identity, bias=W[:, N:N + 1]).then_inc(S["dye" + k], 1)
-        act.wait_ge(S["d" + k], 1)
-        act.wait_ge(S["xs" + k], 1)
-        act.activation(px[:, 0:HB], px[:, 0:HB], F.Identity, bias=W[:, 0:1]).then_inc(S["xd" + k], 1)
-        if h == 1:
-            make_diag("0")
-        dve.wait_ge(S["dd" + k], 1)
-        dve.tensor_tensor_scan(sa[:], Qv, T["jb" + k][:], fN * EPS, A.add, A.add).then_inc(S["den" + k], 1)
-        dve.wait_ge(S["den" + k], 1)
-        dve.reciprocal(rc, den).then_inc(S["rc" + k], 1)
-        dve.wait_ge(S["d" + k], 1)
-        dve.wait_ge(S["e" + k], 1)
-        dve.tensor_tensor(W2[:], d, e, A.mult).then_inc(S["de" + k], 1)
-        dve.wait_ge(S["de" + k], 1)
-        dve.tensor_tensor_scan(sb[:], Pv, W2[:], 0.0, A.add, A.add).then_inc(S["cv" + k], 1)
-        if h == 1:
-            make_diag("1")
-        dve.wait_ge(S["cv" + k], 1)
-        dve.wait_ge(S["rc" + k], 1)
-        dve.wait_ge(S["xd" + k], 1)
-        dve.tensor_scalar(T["u" + k][:], px[:, 0:HB], rc, cv, A.mult, A.mult).then_inc(S["u" + k], 1)
-        dve.wait_ge(S["u" + k], 1)
-        dve.wait_ge(S["dye" + k], 1)
-        dve.tensor_tensor(T["v" + k][:], py[:, 0:HB], T["u" + k][:], A.subtract).then_inc(S["v" + k], 1)
+        if s == 0:
+            for q in (dve, act):
+                q.wait_ge(S["stx" + k], 2)
+                q.wait_ge(S["sty" + k], 2)
+                q.wait_ge(S["arrA" + k], n_a[h])
+                q.wait_ge(S["arrC" + k], n_c[h])
+            dve.tensor_reduce(nsm, Mv, X, A.add, negate=True).then_inc(S["nsm" + k], 1)
+            act.activation(T["ja" + k][:], Yv, F.Copy, scale=-1.0, accum_out=nsy).then_inc(S["nsy" + k], 1)
+        elif s == 1:
+            dve.wait_ge(S["nsm" + k], 1)
+            dve.tensor_scalar(d, Mv, fN, nsm, A.mult, A.add).then_inc(S["d" + k], 1)
+            act.wait_ge(S["nsm" + k], 1)
+            act.activation(T["jb" + k][:], Mv, F.Square, bias=nsm, scale=fN).then_inc(S["dd" + k], 1)
+            act.wait_ge(S["nsy" + k], 1)
+            act.activation(e, Yv, F.Identity, bias=nsy, scale=fN).then_inc(S["e" + k], 1)
+        elif s == 2:
+            dve.wait_ge(S["dd" + k], 1)
+            dve.tensor_tensor_scan(sa[:], Qv, T["jb" + k][:], fN * EPS, A.add, A.add).then_inc(S["den" + k], 1)
+            act.wait_ge(S["e" + k], 1)
+            act.activation(py[:, 0:HB], py[:, 0:HB], F.Identity, bias=W[:, N:N + 1]).then_inc(S["dye" + k], 1)
+        elif s == 3:
+            dve.wait_ge(S["d" + k], 1)
+            dve.wait_ge(S["e" + k], 1)
+            dve.tensor_tensor(W2[:], d, e, A.mult).then_inc(S["de" + k], 1)
+            act.wait_ge(S["d" + k], 1)
+            act.wait_ge(S["xs" + k], 1)
+            act.activation(px[:, 0:HB], px[:, 0:HB], F.Identity, bias=W[:, 0:1]).then_inc(S["xd" + k], 1)
+        elif s == 4:
+            dve.wait_ge(S["den" + k], 1)
+            dve.reciprocal(rc, den).then_inc(S["rc" + k], 1)
+        elif s == 5:
+            dve.wait_ge(S["de" + k], 1)
+            dve.tensor_tensor_scan(sb[:], Pv, W2[:], 0.0, A.add, A.add).then_inc(S["cv" + k], 1)
+            act.wait_ge(S["rc" + k], 1)
+            act.wait_ge(S.idN, 1)
+            act.activation(T["diag" + k][:], T.identN[:], F.Sqrt, scale=sc[:, 2:3]).then_inc(S["diag" + k], 1)
+        elif s == 6:
+            dve.wait_ge(S["cv" + k], 1)
+            dve.wait_ge(S["rc" + k], 1)
+            dve.wait_ge(S["xd" + k], 1)
+            dve.tensor_scalar(T["u" + k][:], px[:, 0:HB], rc, cv, A.mult, A.mult).then_inc(S["u" + k], 1)
+        elif s == 7:
+            dve.wait_ge(S["u" + k], 1)
+            dve.wait_ge(S["dye" + k], 1)
+            dve.tensor_tensor(T["v" + k][:], py[:, 0:HB], T["u" + k][:], A.subtract).then_inc(S["v" + k], 1)
+
+    order = [(s, 0) for s in range(LEAD)]
+    for s in range(STAGES):
+        order.append((s, 1))
+        if s + LEAD < STAGES:
+            order.append((s + LEAD, 0))
+    for s, h in order:
+        stage(s, h)
 
     for h in (0, 1):
         k = str(h)
@@ -200,11 +212,14 @@ def rank_program(g, core, T, topo):
         pe.wait_ge(S["diag" + k], 1)
         pe.matmul(T["po" + k][:, 0:HB], T["v" + k][:], T["diag" + k][:], True, True).then_inc(S["po" + k], 1)
 
-    for h in (0, 1):
+    for h, q in ((0, act), (1, dve)):
         k = str(h)
         c0, c1 = h * HB, (h + 1) * HB
-        dve.wait_ge(S["po" + k], 1)
-        dve.tensor_copy(T["ob" + k][:], T["po" + k][:, 0:HB]).then_inc(S["ob" + k], 1)
+        q.wait_ge(S["po" + k], 1)
+        if q is act:
+            q.activation(T["ob" + k][:], T["po" + k][:, 0:HB], F.Copy).then_inc(S["ob" + k], 1)
+        else:
+            q.tensor_copy(T["ob" + k][:], T["po" + k][:, 0:HB]).then_inc(S["ob" + k], 1)
         sp.wait_ge(S["ob" + k], 1)
         sp.dma_start(T.dx[:, c0:c1], T["ob" + k][:]).then_inc(S["store" + k], 16)
     for h in (0, 1):

@@ -4,14 +4,13 @@ from concourse.mybir import AluOpType, AxisListType, ActivationFunctionType
 N = 12
 EPS = 0.01
 HB = 128
-SLW = (8, 4)
-COL = ((0, 4, 1, 5), (0, 1, 2, 3))
-STAGES = 8
-LEAD = 4
+SLX = 8
+SLY = 4
 
-_PER_HALF = ["ldx", "ldy", "px", "py", "xs", "prod", "stx", "sty", "arrA", "arrC", "nsm", "d", "nsy", "dd", "e",
+_PER_HALF = ["ldx", "ldy", "px", "py", "xs", "prod", "stx", "sty", "arrAY", "arrCY", "nsm", "d", "nsy", "dd", "e",
              "dye", "xd", "den", "rc", "de", "cv", "u", "v", "diag", "po", "ob", "store"]
-SEMAPHORES = ["ms", "cm", "idn", "idN", "sent"] + [n + str(h) for h in (0, 1) for n in _PER_HALF]
+SEMAPHORES = ["msR", "msK", "ms", "cm", "idn", "idN", "sent", "arrAX", "arrCX"] + \
+             [n + str(h) for h in (0, 1) for n in _PER_HALF]
 
 SCRATCH = {
     "xin": ("sbuf", [128, 256], "float32"),
@@ -19,15 +18,14 @@ SCRATCH = {
     "R": ("sbuf", [128, 132], "float32"),
     "ident": ("sbuf", [128, 128], "float32"),
     "identN": ("sbuf", [128, 128], "float32"),
-    "land0": ("sbuf", [128, N * SLW[0]], "float32"),
-    "land1": ("sbuf", [128, N * SLW[1]], "float32"),
+    "LX": ("sbuf", [128, N * SLX], "float32"),
+    "LY0": ("sbuf", [128, N * SLY], "float32"),
+    "LY1": ("sbuf", [128, N * SLY], "float32"),
 }
 for _h in ("0", "1"):
     for _n in ("xs", "jq", "prod", "u", "v", "diag", "ob"):
         SCRATCH[_n + _h] = ("sbuf", [128, HB], "float32")
-    SCRATCH["W" + _h] = ("sbuf", [128, 2 * N], "float32")
-    SCRATCH["W2" + _h] = ("sbuf", [128, N], "float32")
-    for _n in ("ja", "jb", "sa", "sb"):
+    for _n in ("W", "W2", "ja", "jb", "sa", "sb"):
         SCRATCH[_n + _h] = ("sbuf", [128, N], "float32")
     SCRATCH["sc" + _h] = ("sbuf", [128, 12], "float32")
     for _n in ("px", "py", "po"):
@@ -73,138 +71,189 @@ def rank_program(g, core, T, topo):
         rid, pid, _ = topo.addr(q)
         return DstId(rid=rid, pnc=pid)
 
-    for h in (0, 1):
-        c0, c1 = h * HB, (h + 1) * HB
-        sp.dma_start(T.xin[:, c0:c1], T.x[:, c0:c1]).then_inc(S["ldx%d" % h], 16)
-        act.dma_start(T.dyin[:, c0:c1], T.dy[:, c0:c1]).then_inc(S["ldy%d" % h], 16)
+    sp.dma_start(T.xin[:, 0:HB], T.x[:, 0:HB]).then_inc(S.ldx0, 16)
+    act.dma_start(T.xin[:, HB:2 * HB], T.x[:, HB:2 * HB]).then_inc(S.ldx1, 16)
+    sp.dma_start(T.dyin[:, 0:HB], T.dy[:, 0:HB]).then_inc(S.ldy0, 16)
+    act.dma_start(T.dyin[:, HB:2 * HB], T.dy[:, HB:2 * HB]).then_inc(S.ldy1, 16)
 
-    dve.memset(T.R[:, 0:HB], -1.0 / 128.0).then_inc(S.ms, 1)
-    dve.memset(T.R[:, HB:HB + 1], 1.0 / (128.0 * N)).then_inc(S.ms, 1)
-    dve.memset(T.land0[:, 2:4], 0.0).then_inc(S.ms, 1)
-    dve.memset(T.land0[:, 6:8], 0.0).then_inc(S.ms, 1)
-    g.wait_ge(S.ms, 4)
+    dve.memset(T.R[:, 0:HB], -1.0 / 128.0).then_inc(S.msR, 1)
+    dve.memset(T.R[:, HB:HB + 1], 1.0 / (128.0 * N)).then_inc(S.msK, 1)
+    dve.memset(T.R[:, HB + 1:HB + 2], 1.0 / 128.0).then_inc(S.msK, 1)
+    dve.memset(T.LX[:, 2:4], 0.0).then_inc(S.ms, 1)
+    dve.memset(T.LX[:, 6:8], 0.0).then_inc(S.ms, 1)
+    dve.memset(T.LY0[:, 2:4], 0.0).then_inc(S.ms, 1)
+    dve.memset(T.LY1[:, 2:4], 0.0).then_inc(S.ms, 1)
+    g.wait_ge(S.msR, 1)
     g.affine_select(T.R[:, 0:HB], T.R[:, 0:HB], [[-1, HB]], A.not_equal, 127.0 / 128.0, 0, 1).then_inc(S.cm, 1)
     dve.wait_ge(S.cm, 1)
     dve.tensor_scalar(T.ident[:], T.R[:, 0:HB], 1.0 / 128.0, None, A.add).then_inc(S.idn, 1)
 
+    RW = HB + 2
     pe.wait_ge(S.cm, 1)
+    pe.wait_ge(S.msK, 2)
     for h in (0, 1):
         k = str(h)
-        c0, c1 = h * HB, (h + 1) * HB
-        cM, cY, cQ, cP = COL[h]
-        px, py, land = T["px" + k], T["py" + k], T["land" + k]
         pe.wait_ge(S["ldx" + k], 16)
-        pe.matmul(px[:, 0:HB + 1], T.xin[:, c0:c1], T.R[:, 0:HB + 1], True, True).then_inc(S["px" + k], 1)
+        pe.matmul(T["px" + k][:, 0:RW], T.xin[:, h * HB:(h + 1) * HB], T.R[:, 0:RW], True, True).then_inc(S["px" + k], 1)
+    for h in (0, 1):
+        k = str(h)
         pe.wait_ge(S["ldy" + k], 16)
-        pe.matmul(py[:, 0:HB + 1], T.dyin[:, c0:c1], T.R[:, 0:HB + 1], True, True).then_inc(S["py" + k], 1)
+        pe.matmul(T["py" + k][:, 0:RW], T.dyin[:, h * HB:(h + 1) * HB], T.R[:, 0:RW], True, True).then_inc(S["py" + k], 1)
+    for h in (0, 1):
+        k = str(h)
+        px = T["px" + k]
         act.wait_ge(S["px" + k], 1)
-        act.activation(T["xs" + k][:], px[:, 0:HB], F.Copy, scale=1.0 / 128.0).then_inc(S["xs" + k], 1)
         act.activation(T["jq" + k][:], px[:, 0:HB], F.Square, scale=2.0 ** -3.5,
-                       accum_out=land[:, cQ:cQ + 1]).then_inc(S["stx" + k], 1)
-        act.activation(land[:, cM:cM + 1], px[:, HB:HB + 1], F.Copy).then_inc(S["stx" + k], 1)
+                       accum_out=T.LX[:, 4 * h + 1:4 * h + 2]).then_inc(S["stx" + k], 1)
+        act.activation(T.LX[:, 4 * h:4 * h + 1], px[:, HB:HB + 1], F.Copy).then_inc(S["stx" + k], 1)
+        act.activation(T["xs" + k][:], px[:, 0:HB], F.Copy, scale=1.0 / 128.0).then_inc(S["xs" + k], 1)
+    for h in (0, 1):
+        k = str(h)
+        py, LY = T["py" + k], T["LY" + k]
         dve.wait_ge(S["py" + k], 1)
         dve.wait_ge(S["xs" + k], 1)
         dve.tensor_tensor(T["prod" + k][:], py[:, 0:HB], T["xs" + k][:], A.mult).then_inc(S["prod" + k], 1)
+        dve.tensor_copy(LY[:, 0:1], py[:, HB + 1:HB + 2]).then_inc(S["sty" + k], 1)
         dve.wait_ge(S["prod" + k], 1)
-        dve.tensor_reduce(land[:, cP:cP + 1], T["prod" + k][:], X, A.add).then_inc(S["sty" + k], 1)
-        act.wait_ge(S["prod" + k], 1)
-        act.activation(land[:, cY:cY + 1], py[:, HB:HB + 1], F.Copy).then_inc(S["sty" + k], 1)
+        dve.tensor_reduce(LY[:, 1:2], T["prod" + k][:], X, A.add).then_inc(S["sty" + k], 1)
 
     act.wait_ge(S.idn, 1)
     act.activation(T.identN[:], T.ident[:], F.Sqrt, scale=float(N * N)).then_inc(S.idN, 1)
+    for h in (0, 1):
+        k = str(h)
+        act.wait_ge(S["sty" + k], 2)
+        act.activation(T["py" + k][:, 0:HB], T["py" + k][:, 0:HB], F.Identity,
+                       bias=T["LY" + k][:, 0:1]).then_inc(S["e" + k], 1)
 
-    def send(h, dests, mask, lo, hi, sem):
-        land = T["land%d" % h]
+    def send(land, slw, dests, mask, lo, hi, sem):
         if dests is far:
-            base = [SLW[h] * (1 + fellows(q).index(core)) for q in dests]
+            base = [slw * (1 + fellows(q).index(core)) for q in dests]
         else:
-            base = [SLW[h] * grp * (1 + neighbours(q).index(core)) for q in dests]
+            base = [slw * grp * (1 + neighbours(q).index(core)) for q in dests]
         g.remote_dma_fused([RemoteDMATransfer(dst_ids=[dst(q) for q in dests], dma_engine_mask=mask, remote_sem=sem,
                                               srcs=[land[:, lo:hi]], dsts=[land[:, b + lo:b + hi] for b in base],
                                               alu_op=0)], local_sem=S.sent)
         return _bits(mask)
 
     bf, bn, bs = _bits(mask_far), _bits(mask_near), _bits(mask_side)
+    n_ax, n_ay, n_c, n_cx = 2 * len(far) * bf, len(far) * bf, len(near) * bn, len(near) * (bs + bn)
     sent = 0
+    g.wait_ge(S.ms, 4)
     g.wait_ge(S.stx0, 2)
-    sent += send(0, far, mask_far, 0, 4, S.arrA0)
-    g.wait_ge(S.sty0, 2)
-    sent += send(0, far, mask_far, 4, 8, S.arrA0)
-    sent += send(0, near, mask_side, 0, 4, S.arrC0)
+    sent += send(T.LX, SLX, far, mask_far, 0, 4, S.arrAX)
     g.wait_ge(S.stx1, 2)
+    sent += send(T.LX, SLX, far, mask_far, 4, 8, S.arrAX)
+    sent += send(T.LX, SLX, near, mask_side, 0, SLX, S.arrCX)
+    g.wait_ge(S.sty0, 2)
+    sent += send(T.LY0, SLY, far, mask_far, 0, SLY, S.arrAY0)
     g.wait_ge(S.sty1, 2)
-    sent += send(1, far, mask_far, 0, 4, S.arrA1)
-    n_a = (2 * len(far) * bf, len(far) * bf)
-    g.wait_ge(S.arrA0, n_a[0])
-    sent += send(0, near, mask_near, 4, grp * SLW[0], S.arrC0)
-    g.wait_ge(S.arrA1, n_a[1])
-    sent += send(1, near, mask_near, 0, grp * SLW[1], S.arrC1)
-    n_c = (len(near) * (bs + bn), len(near) * bn)
+    sent += send(T.LY1, SLY, far, mask_far, 0, SLY, S.arrAY1)
+    g.wait_ge(S.arrAX, n_ax)
+    sent += send(T.LX, SLX, near, mask_near, SLX, grp * SLX, S.arrCX)
+    g.wait_ge(S.arrAY0, n_ay)
+    sent += send(T.LY0, SLY, near, mask_near, 0, grp * SLY, S.arrCY0)
+    g.wait_ge(S.arrAY1, n_ay)
+    sent += send(T.LY1, SLY, near, mask_near, 0, grp * SLY, S.arrCY1)
     g.wait_ge(S.sent, sent)
 
     fN = float(N)
 
-    def stage(s, h):
+    def names(h):
         k = str(h)
-        px, py, land = T["px" + k], T["py" + k], T["land" + k]
-        W, W2, sc, sa, sb = T["W" + k], T["W2" + k], T["sc" + k], T["sa" + k], T["sb" + k]
-        Mv, Yv, Qv, Pv = (land[:, i:N * SLW[h]:SLW[h]] for i in COL[h])
-        nsm, nsy, rc = (sc[:, i:i + 1] for i in range(3))
-        den, cv = sa[:, N - 1:N], sb[:, N - 1:N]
-        d, e = W[:, 0:N], W[:, N:2 * N]
-        if s == 0:
-            for q in (dve, act):
-                q.wait_ge(S["stx" + k], 2)
-                q.wait_ge(S["sty" + k], 2)
-                q.wait_ge(S["arrA" + k], n_a[h])
-                q.wait_ge(S["arrC" + k], n_c[h])
-            dve.tensor_reduce(nsm, Mv, X, A.add, negate=True).then_inc(S["nsm" + k], 1)
-            act.activation(T["ja" + k][:], Yv, F.Copy, scale=-1.0, accum_out=nsy).then_inc(S["nsy" + k], 1)
-        elif s == 1:
-            dve.wait_ge(S["nsm" + k], 1)
-            dve.tensor_scalar(d, Mv, fN, nsm, A.mult, A.add).then_inc(S["d" + k], 1)
-            act.wait_ge(S["nsm" + k], 1)
-            act.activation(T["jb" + k][:], Mv, F.Square, bias=nsm, scale=fN).then_inc(S["dd" + k], 1)
-            act.wait_ge(S["nsy" + k], 1)
-            act.activation(e, Yv, F.Identity, bias=nsy, scale=fN).then_inc(S["e" + k], 1)
-        elif s == 2:
-            dve.wait_ge(S["dd" + k], 1)
-            dve.tensor_tensor_scan(sa[:], Qv, T["jb" + k][:], fN * EPS, A.add, A.add).then_inc(S["den" + k], 1)
-            act.wait_ge(S["e" + k], 1)
-            act.activation(py[:, 0:HB], py[:, 0:HB], F.Identity, bias=W[:, N:N + 1]).then_inc(S["dye" + k], 1)
-        elif s == 3:
-            dve.wait_ge(S["d" + k], 1)
-            dve.wait_ge(S["e" + k], 1)
-            dve.tensor_tensor(W2[:], d, e, A.mult).then_inc(S["de" + k], 1)
-            act.wait_ge(S["d" + k], 1)
-            act.wait_ge(S["xs" + k], 1)
-            act.activation(px[:, 0:HB], px[:, 0:HB], F.Identity, bias=W[:, 0:1]).then_inc(S["xd" + k], 1)
-        elif s == 4:
-            dve.wait_ge(S["den" + k], 1)
-            dve.reciprocal(rc, den).then_inc(S["rc" + k], 1)
-        elif s == 5:
-            dve.wait_ge(S["de" + k], 1)
-            dve.tensor_tensor_scan(sb[:], Pv, W2[:], 0.0, A.add, A.add).then_inc(S["cv" + k], 1)
-            act.wait_ge(S["rc" + k], 1)
-            act.wait_ge(S.idN, 1)
-            act.activation(T["diag" + k][:], T.identN[:], F.Sqrt, scale=sc[:, 2:3]).then_inc(S["diag" + k], 1)
-        elif s == 6:
-            dve.wait_ge(S["cv" + k], 1)
-            dve.wait_ge(S["rc" + k], 1)
-            dve.wait_ge(S["xd" + k], 1)
-            dve.tensor_scalar(T["u" + k][:], px[:, 0:HB], rc, cv, A.mult, A.mult).then_inc(S["u" + k], 1)
-        elif s == 7:
-            dve.wait_ge(S["u" + k], 1)
-            dve.wait_ge(S["dye" + k], 1)
-            dve.tensor_tensor(T["v" + k][:], py[:, 0:HB], T["u" + k][:], A.subtract).then_inc(S["v" + k], 1)
+        sc = T["sc" + k]
+        return dict(k=k, px=T["px" + k], py=T["py" + k], LY=T["LY" + k], d=T["W" + k], W2=T["W2" + k],
+                    sa=T["sa" + k], sb=T["sb" + k], jb=T["jb" + k], ja=T["ja" + k],
+                    Mv=T.LX[:, 4 * h:N * SLX:SLX], Qv=T.LX[:, 4 * h + 1:N * SLX:SLX],
+                    Yv=T["LY" + k][:, 0:N * SLY:SLY], Pv=T["LY" + k][:, 1:N * SLY:SLY],
+                    nsm=sc[:, 0:1], nsy=sc[:, 1:2], rc=sc[:, 2:3],
+                    den=T["sa" + k][:, N - 1:N], cv=T["sb" + k][:, N - 1:N])
 
-    order = [(s, 0) for s in range(LEAD)]
-    for s in range(STAGES):
-        order.append((s, 1))
-        if s + LEAD < STAGES:
-            order.append((s + LEAD, 0))
-    for s, h in order:
-        stage(s, h)
+    def x_landed(q):
+        for nm, n in (("stx0", 2), ("stx1", 2), ("arrAX", n_ax), ("arrCX", n_cx)):
+            q.wait_ge(S[nm], n)
+
+    def y_landed(q, k):
+        for nm, n in (("sty" + k, 2), ("arrAY" + k, n_ay), ("arrCY" + k, n_c)):
+            q.wait_ge(S[nm], n)
+
+    def v_nsm(h):
+        c = names(h)
+        x_landed(dve)
+        dve.tensor_reduce(c["nsm"], c["Mv"], X, A.add, negate=True).then_inc(S["nsm" + c["k"]], 1)
+
+    def v_d(h):
+        c = names(h)
+        dve.wait_ge(S["nsm" + c["k"]], 1)
+        dve.tensor_scalar(c["d"][:], c["Mv"], fN, c["nsm"], A.mult, A.add).then_inc(S["d" + c["k"]], 1)
+
+    def v_den(h):
+        c = names(h)
+        dve.wait_ge(S["dd" + c["k"]], 1)
+        dve.tensor_tensor_scan(c["sa"][:], c["Qv"], c["jb"][:], fN * EPS, A.add, A.add).then_inc(S["den" + c["k"]], 1)
+
+    def v_rc(h):
+        c = names(h)
+        dve.wait_ge(S["den" + c["k"]], 1)
+        dve.reciprocal(c["rc"], c["den"]).then_inc(S["rc" + c["k"]], 1)
+
+    def v_de(h):
+        c = names(h)
+        y_landed(dve, c["k"])
+        dve.wait_ge(S["d" + c["k"]], 1)
+        dve.tensor_tensor(c["W2"][:], c["d"][:], c["Yv"], A.mult).then_inc(S["de" + c["k"]], 1)
+
+    def v_cv(h):
+        c = names(h)
+        dve.wait_ge(S["de" + c["k"]], 1)
+        dve.tensor_tensor_scan(c["sb"][:], c["Pv"], c["W2"][:], 0.0, A.add, A.add).then_inc(S["cv" + c["k"]], 1)
+
+    def v_u(h):
+        c = names(h)
+        for nm in ("cv", "rc", "xd"):
+            dve.wait_ge(S[nm + c["k"]], 1)
+        dve.tensor_scalar(T["u" + c["k"]][:], c["px"][:, 0:HB], c["rc"], c["cv"], A.mult, A.mult).then_inc(S["u" + c["k"]], 1)
+
+    def v_v(h):
+        c = names(h)
+        dve.wait_ge(S["u" + c["k"]], 1)
+        dve.wait_ge(S["dye" + c["k"]], 1)
+        dve.tensor_tensor(T["v" + c["k"]][:], c["py"][:, 0:HB], T["u" + c["k"]][:], A.subtract).then_inc(S["v" + c["k"]], 1)
+
+    def s_dd(h):
+        c = names(h)
+        x_landed(act)
+        act.wait_ge(S["nsm" + c["k"]], 1)
+        act.activation(c["jb"][:], c["Mv"], F.Square, bias=c["nsm"], scale=fN).then_inc(S["dd" + c["k"]], 1)
+
+    def s_xd(h):
+        c = names(h)
+        act.wait_ge(S["d" + c["k"]], 1)
+        act.wait_ge(S["xs" + c["k"]], 1)
+        act.activation(c["px"][:, 0:HB], c["px"][:, 0:HB], F.Identity, bias=c["d"][:, 0:1]).then_inc(S["xd" + c["k"]], 1)
+
+    def s_nsy(h):
+        c = names(h)
+        y_landed(act, c["k"])
+        act.activation(c["ja"][:], c["Yv"], F.Copy, scale=-1.0 / fN, accum_out=c["nsy"]).then_inc(S["nsy" + c["k"]], 1)
+
+    def s_dye(h):
+        c = names(h)
+        act.wait_ge(S["nsy" + c["k"]], 1)
+        act.wait_ge(S["e" + c["k"]], 1)
+        act.activation(c["py"][:, 0:HB], c["py"][:, 0:HB], F.Identity, bias=c["nsy"]).then_inc(S["dye" + c["k"]], 1)
+
+    def s_diag(h):
+        c = names(h)
+        act.wait_ge(S["rc" + c["k"]], 1)
+        act.wait_ge(S.idN, 1)
+        act.activation(T["diag" + c["k"]][:], T.identN[:], F.Sqrt, scale=c["rc"]).then_inc(S["diag" + c["k"]], 1)
+
+    for f, h in ((v_nsm, 0), (v_nsm, 1), (v_d, 0), (v_d, 1), (v_den, 0), (v_den, 1), (v_de, 0), (v_rc, 0), (v_cv, 0),
+                 (v_rc, 1), (v_de, 1), (v_u, 0), (v_cv, 1), (v_v, 0), (v_u, 1), (v_v, 1)):
+        f(h)
+    for f, h in ((s_dd, 0), (s_dd, 1), (s_xd, 0), (s_xd, 1), (s_nsy, 0), (s_dye, 0), (s_nsy, 1), (s_diag, 0),
+                 (s_dye, 1), (s_diag, 1)):
+        f(h)
 
     for h in (0, 1):
         k = str(h)

@@ -4,12 +4,14 @@ from concourse.mybir import AluOpType, AxisListType, ActivationFunctionType
 N = 12
 EPS = 0.01
 HB = 128
+HQ = 64
 SLX = 8
+QCOL = (6, 5)
 SLY = 4
 
 _PER_HALF = ["ldx", "ldy", "px", "py", "xs", "prod", "stx", "sty", "arrAY", "arrCY", "nsm", "d", "nsy", "dd", "e",
              "dye", "xd", "den", "rc", "de", "cv", "u", "v", "diag", "po", "ob", "store"]
-SEMAPHORES = ["msR", "msK", "ms", "cm", "idn", "idN", "sent", "arrAX", "arrCX"] + \
+SEMAPHORES = ["msR", "msK", "ms", "cm", "idn", "idN", "sent", "arrAX", "arrCX", "pm", "stm0", "pq"] + \
              [n + str(h) for h in (0, 1) for n in _PER_HALF]
 
 SCRATCH = {
@@ -21,6 +23,8 @@ SCRATCH = {
     "LX": ("sbuf", [128, N * SLX], "float32"),
     "LY0": ("sbuf", [128, N * SLY], "float32"),
     "LY1": ("sbuf", [128, N * SLY], "float32"),
+    "pm": ("psum", [128, 512], "float32"),
+    "pq": ("psum", [128, 512], "float32"),
 }
 for _h in ("0", "1"):
     for _n in ("xs", "jq", "prod", "u", "v", "diag", "ob"):
@@ -79,8 +83,8 @@ def rank_program(g, core, T, topo):
     dve.memset(T.R[:, 0:HB], -1.0 / 128.0).then_inc(S.msR, 1)
     dve.memset(T.R[:, HB:HB + 1], 1.0 / (128.0 * N)).then_inc(S.msK, 1)
     dve.memset(T.R[:, HB + 1:HB + 2], 1.0 / 128.0).then_inc(S.msK, 1)
-    dve.memset(T.LX[:, 2:4], 0.0).then_inc(S.ms, 1)
-    dve.memset(T.LX[:, 6:8], 0.0).then_inc(S.ms, 1)
+    dve.memset(T.LX[:, 1:4], 0.0).then_inc(S.ms, 1)
+    dve.memset(T.LX[:, 7:8], 0.0).then_inc(S.ms, 1)
     dve.memset(T.LY0[:, 2:4], 0.0).then_inc(S.ms, 1)
     dve.memset(T.LY1[:, 2:4], 0.0).then_inc(S.ms, 1)
     g.wait_ge(S.msR, 1)
@@ -89,23 +93,29 @@ def rank_program(g, core, T, topo):
     dve.tensor_scalar(T.ident[:], T.R[:, 0:HB], 1.0 / 128.0, None, A.add).then_inc(S.idn, 1)
 
     RW = HB + 2
-    pe.wait_ge(S.cm, 1)
     pe.wait_ge(S.msK, 2)
+    pe.wait_ge(S.ldx0, 16)
+    pe.matmul(T.pm[:, 0:1], T.xin[:, 0:HB], T.R[:, HB:HB + 1], True, True).then_inc(S.pm, 1)
+    pe.wait_ge(S.cm, 1)
     for h in (0, 1):
         k = str(h)
+        w = HB if h == 0 else RW
         pe.wait_ge(S["ldx" + k], 16)
-        pe.matmul(T["px" + k][:, 0:RW], T.xin[:, h * HB:(h + 1) * HB], T.R[:, 0:RW], True, True).then_inc(S["px" + k], 1)
+        pe.matmul(T["px" + k][:, 0:w], T.xin[:, h * HB:(h + 1) * HB], T.R[:, 0:w], True, True).then_inc(S["px" + k], 1)
     for h in (0, 1):
         k = str(h)
         pe.wait_ge(S["ldy" + k], 16)
         pe.matmul(T["py" + k][:, 0:RW], T.dyin[:, h * HB:(h + 1) * HB], T.R[:, 0:RW], True, True).then_inc(S["py" + k], 1)
+    act.wait_ge(S.pm, 1)
+    act.activation(T.LX[:, 0:1], T.pm[:, 0:1], F.Copy).then_inc(S.stm0, 1)
     for h in (0, 1):
         k = str(h)
         px = T["px" + k]
         act.wait_ge(S["px" + k], 1)
         act.activation(T["jq" + k][:], px[:, 0:HB], F.Square, scale=2.0 ** -3.5,
-                       accum_out=T.LX[:, 4 * h + 1:4 * h + 2]).then_inc(S["stx" + k], 1)
-        act.activation(T.LX[:, 4 * h:4 * h + 1], px[:, HB:HB + 1], F.Copy).then_inc(S["stx" + k], 1)
+                       accum_out=T.LX[:, QCOL[h]:QCOL[h] + 1]).then_inc(S["stx" + k], 1)
+        if h == 1:
+            act.activation(T.LX[:, 4:5], px[:, HB:HB + 1], F.Copy).then_inc(S.stx1, 1)
         act.activation(T["xs" + k][:], px[:, 0:HB], F.Copy, scale=1.0 / 128.0).then_inc(S["xs" + k], 1)
     for h in (0, 1):
         k = str(h)
@@ -139,8 +149,9 @@ def rank_program(g, core, T, topo):
     n_ax, n_ay, n_c, n_cx = 2 * len(far) * bf, len(far) * bf, len(near) * bn, len(near) * (bs + bn)
     sent = 0
     g.wait_ge(S.ms, 4)
-    g.wait_ge(S.stx0, 2)
+    g.wait_ge(S.stm0, 1)
     sent += send(T.LX, SLX, far, mask_far, 0, 4, S.arrAX)
+    g.wait_ge(S.stx0, 1)
     g.wait_ge(S.stx1, 2)
     sent += send(T.LX, SLX, far, mask_far, 4, 8, S.arrAX)
     sent += send(T.LX, SLX, near, mask_side, 0, SLX, S.arrCX)
@@ -163,13 +174,13 @@ def rank_program(g, core, T, topo):
         sc = T["sc" + k]
         return dict(k=k, px=T["px" + k], py=T["py" + k], LY=T["LY" + k], d=T["W" + k], W2=T["W2" + k],
                     sa=T["sa" + k], sb=T["sb" + k], jb=T["jb" + k], ja=T["ja" + k],
-                    Mv=T.LX[:, 4 * h:N * SLX:SLX], Qv=T.LX[:, 4 * h + 1:N * SLX:SLX],
+                    Mv=T.LX[:, 4 * h:N * SLX:SLX], Qv=T.LX[:, QCOL[h]:N * SLX:SLX],
                     Yv=T["LY" + k][:, 0:N * SLY:SLY], Pv=T["LY" + k][:, 1:N * SLY:SLY],
                     nsm=sc[:, 0:1], nsy=sc[:, 1:2], rc=sc[:, 2:3],
                     den=T["sa" + k][:, N - 1:N], cv=T["sb" + k][:, N - 1:N])
 
     def x_landed(q):
-        for nm, n in (("stx0", 2), ("stx1", 2), ("arrAX", n_ax), ("arrCX", n_cx)):
+        for nm, n in (("stm0", 1), ("stx0", 1), ("stx1", 2), ("arrAX", n_ax), ("arrCX", n_cx)):
             q.wait_ge(S[nm], n)
 
     def y_landed(q, k):
@@ -255,21 +266,23 @@ def rank_program(g, core, T, topo):
                  (s_dye, 1), (s_diag, 1)):
         f(h)
 
-    for h in (0, 1):
-        k = str(h)
-        pe.wait_ge(S["v" + k], 1)
-        pe.wait_ge(S["diag" + k], 1)
-        pe.matmul(T["po" + k][:, 0:HB], T["v" + k][:], T["diag" + k][:], True, True).then_inc(S["po" + k], 1)
+    pe.wait_ge(S.v0, 1)
+    pe.wait_ge(S.diag0, 1)
+    pe.matmul(T.po0[:, 0:HB], T.v0[:], T.diag0[:], True, True).then_inc(S.po0, 1)
+    pe.wait_ge(S.v1, 1)
+    pe.wait_ge(S.diag1, 1)
+    pe.matmul(T.po1[:, 0:HQ], T.v1[:], T.diag1[:, 0:HQ], True, True).then_inc(S.po1, 1)
+    pe.matmul(T.pq[:, 0:HQ], T.v1[:], T.diag1[:, HQ:HB], True, True).then_inc(S.pq, 1)
 
-    for h, q in ((0, act), (1, dve)):
-        k = str(h)
-        c0, c1 = h * HB, (h + 1) * HB
-        q.wait_ge(S["po" + k], 1)
-        if q is act:
-            q.activation(T["ob" + k][:], T["po" + k][:, 0:HB], F.Copy).then_inc(S["ob" + k], 1)
-        else:
-            q.tensor_copy(T["ob" + k][:], T["po" + k][:, 0:HB]).then_inc(S["ob" + k], 1)
-        sp.wait_ge(S["ob" + k], 1)
-        sp.dma_start(T.dx[:, c0:c1], T["ob" + k][:]).then_inc(S["store" + k], 16)
+    act.wait_ge(S.po0, 1)
+    act.activation(T.ob0[:], T.po0[:, 0:HB], F.Copy).then_inc(S.ob0, 1)
+    sp.wait_ge(S.ob0, 1)
+    sp.dma_start(T.dx[:, 0:HB], T.ob0[:]).then_inc(S.store0, 16)
+    act.wait_ge(S.po1, 1)
+    act.activation(T.ob1[:, 0:HQ], T.po1[:, 0:HQ], F.Copy).then_inc(S.ob1, 1)
+    dve.wait_ge(S.pq, 1)
+    dve.tensor_copy(T.ob1[:, HQ:HB], T.pq[:, 0:HQ]).then_inc(S.ob1, 1)
+    sp.wait_ge(S.ob1, 2)
+    sp.dma_start(T.dx[:, HB:2 * HB], T.ob1[:]).then_inc(S.store1, 16)
     for h in (0, 1):
         sp.wait_ge(S["store%d" % h], 16)

from concourse.bass import DstId, RemoteDMATransfer
from concourse.mybir import AluOpType, AxisListType, ActivationFunctionType

N = 12
EPS = 0.01
HB = 128
HQ = 64
SLX = 8
QCOL = (6, 5)
SLY = 4

_PER_HALF = ["ldx", "ldy", "px", "py", "xs", "prod", "stx", "sty", "arrAY", "arrCY", "nsm", "d", "nsy", "dd", "e",
             "dye", "xd", "den", "rc", "de", "cv", "u", "v", "diag", "po", "ob", "store"]
SEMAPHORES = ["msR", "msK", "ms", "cm", "idn", "idN", "sent", "arrAX", "arrCX", "pm", "stm0", "pq"] + \
             [n + str(h) for h in (0, 1) for n in _PER_HALF]

SCRATCH = {
    "xin": ("sbuf", [128, 256], "float32"),
    "dyin": ("sbuf", [128, 256], "float32"),
    "R": ("sbuf", [128, 132], "float32"),
    "ident": ("sbuf", [128, 128], "float32"),
    "identN": ("sbuf", [128, 128], "float32"),
    "LX": ("sbuf", [128, N * SLX], "float32"),
    "LY0": ("sbuf", [128, N * SLY], "float32"),
    "LY1": ("sbuf", [128, N * SLY], "float32"),
    "pm": ("psum", [128, 512], "float32"),
    "pq": ("psum", [128, 512], "float32"),
}
for _h in ("0", "1"):
    for _n in ("xs", "jq", "prod", "u", "v", "diag", "ob"):
        SCRATCH[_n + _h] = ("sbuf", [128, HB], "float32")
    for _n in ("W", "W2", "ja", "jb", "sa", "sb"):
        SCRATCH[_n + _h] = ("sbuf", [128, N], "float32")
    SCRATCH["sc" + _h] = ("sbuf", [128, 12], "float32")
    for _n in ("px", "py", "po"):
        SCRATCH[_n + _h] = ("psum", [128, 512], "float32")


def _bits(mask):
    return bin(mask).count("1")


def rank_program(g, core, T, topo):
    if T.rank_of(core) is None:
        return
    ranks = list(T.cores)
    A, X, F = AluOpType, AxisListType.X, ActivationFunctionType
    S = T.sem
    pe, dve, act, sp = g.tensor, g.vector, g.scalar, g.sync

    def place(c):
        same = [q for q in ranks if topo.chip(q) == topo.chip(c) and topo.die(q) == topo.die(c)]
        return (topo.die(c), same.index(c))

    def fellows(c):
        return [q for q in ranks if topo.chip(q) != topo.chip(c) and place(q) == place(c)]

    def neighbours(c):
        return [q for q in ranks if topo.chip(q) == topo.chip(c) and q != c]

    far, near = fellows(core), neighbours(core)
    for q in far + near:
        assert topo.may_write(core, q)
    mask_far = topo.mask(core, far[0])
    for q in far:
        mask_far &= topo.mask(core, q)
    mask_near = topo.mask(core, near[0])
    for q in near:
        mask_near &= topo.mask(core, q)
    mask_side = mask_near & ~mask_far
    grp = 1 + len(far)
    assert grp * (1 + len(near)) == N

    def dst(q):
        rid, pid, _ = topo.addr(q)
        return DstId(rid=rid, pnc=pid)

    sp.dma_start(T.xin[:, 0:HB], T.x[:, 0:HB]).then_inc(S.ldx0, 16)
    act.dma_start(T.xin[:, HB:2 * HB], T.x[:, HB:2 * HB]).then_inc(S.ldx1, 16)
    sp.dma_start(T.dyin[:, 0:HB], T.dy[:, 0:HB]).then_inc(S.ldy0, 16)
    act.dma_start(T.dyin[:, HB:2 * HB], T.dy[:, HB:2 * HB]).then_inc(S.ldy1, 16)

    dve.memset(T.R[:, 0:HB], -1.0 / 128.0).then_inc(S.msR, 1)
    dve.memset(T.R[:, HB:HB + 1], 1.0 / (128.0 * N)).then_inc(S.msK, 1)
    dve.memset(T.R[:, HB + 1:HB + 2], 1.0 / 128.0).then_inc(S.msK, 1)
    dve.memset(T.LX[:, 1:4], 0.0).then_inc(S.ms, 1)
    dve.memset(T.LX[:, 7:8], 0.0).then_inc(S.ms, 1)
    dve.memset(T.LY0[:, 2:4], 0.0).then_inc(S.ms, 1)
    dve.memset(T.LY1[:, 2:4], 0.0).then_inc(S.ms, 1)
    g.wait_ge(S.msR, 1)
    g.affine_select(T.R[:, 0:HB], T.R[:, 0:HB], [[-1, HB]], A.not_equal, 127.0 / 128.0, 0, 1).then_inc(S.cm, 1)
    dve.wait_ge(S.cm, 1)
    dve.tensor_scalar(T.ident[:], T.R[:, 0:HB], 1.0 / 128.0, None, A.add).then_inc(S.idn, 1)

    RW = HB + 2
    pe.wait_ge(S.msK, 2)
    pe.wait_ge(S.ldx0, 16)
    pe.matmul(T.pm[:, 0:1], T.xin[:, 0:HB], T.R[:, HB:HB + 1], True, True).then_inc(S.pm, 1)
    pe.wait_ge(S.cm, 1)
    for h in (0, 1):
        k = str(h)
        w = HB if h == 0 else RW
        pe.wait_ge(S["ldx" + k], 16)
        pe.matmul(T["px" + k][:, 0:w], T.xin[:, h * HB:(h + 1) * HB], T.R[:, 0:w], True, True).then_inc(S["px" + k], 1)
    for h in (0, 1):
        k = str(h)
        pe.wait_ge(S["ldy" + k], 16)
        pe.matmul(T["py" + k][:, 0:RW], T.dyin[:, h * HB:(h + 1) * HB], T.R[:, 0:RW], True, True).then_inc(S["py" + k], 1)
    act.wait_ge(S.pm, 1)
    act.activation(T.LX[:, 0:1], T.pm[:, 0:1], F.Copy).then_inc(S.stm0, 1)
    for h in (0, 1):
        k = str(h)
        px = T["px" + k]
        act.wait_ge(S["px" + k], 1)
        act.activation(T["jq" + k][:], px[:, 0:HB], F.Square, scale=2.0 ** -3.5,
                       accum_out=T.LX[:, QCOL[h]:QCOL[h] + 1]).then_inc(S["stx" + k], 1)
        if h == 1:
            act.activation(T.LX[:, 4:5], px[:, HB:HB + 1], F.Copy).then_inc(S.stx1, 1)
        act.activation(T["xs" + k][:], px[:, 0:HB], F.Copy, scale=1.0 / 128.0).then_inc(S["xs" + k], 1)
    for h in (0, 1):
        k = str(h)
        py, LY = T["py" + k], T["LY" + k]
        dve.wait_ge(S["py" + k], 1)
        dve.wait_ge(S["xs" + k], 1)
        dve.tensor_tensor(T["prod" + k][:], py[:, 0:HB], T["xs" + k][:], A.mult).then_inc(S["prod" + k], 1)
        dve.tensor_copy(LY[:, 0:1], py[:, HB + 1:HB + 2]).then_inc(S["sty" + k], 1)
        dve.wait_ge(S["prod" + k], 1)
        dve.tensor_reduce(LY[:, 1:2], T["prod" + k][:], X, A.add).then_inc(S["sty" + k], 1)

    act.wait_ge(S.idn, 1)
    act.activation(T.identN[:], T.ident[:], F.Sqrt, scale=float(N * N)).then_inc(S.idN, 1)
    for h in (0, 1):
        k = str(h)
        act.wait_ge(S["sty" + k], 2)
        act.activation(T["py" + k][:, 0:HB], T["py" + k][:, 0:HB], F.Identity,
                       bias=T["LY" + k][:, 0:1]).then_inc(S["e" + k], 1)

    def send(land, slw, dests, mask, lo, hi, sem):
        if dests is far:
            base = [slw * (1 + fellows(q).index(core)) for q in dests]
        else:
            base = [slw * grp * (1 + neighbours(q).index(core)) for q in dests]
        g.remote_dma_fused([RemoteDMATransfer(dst_ids=[dst(q) for q in dests], dma_engine_mask=mask, remote_sem=sem,
                                              srcs=[land[:, lo:hi]], dsts=[land[:, b + lo:b + hi] for b in base],
                                              alu_op=0)], local_sem=S.sent)
        return _bits(mask)

    bf, bn, bs = _bits(mask_far), _bits(mask_near), _bits(mask_side)
    n_ax, n_ay, n_c, n_cx = 2 * len(far) * bf, len(far) * bf, len(near) * bn, len(near) * (bs + bn)
    sent = 0
    g.wait_ge(S.ms, 4)
    g.wait_ge(S.stm0, 1)
    sent += send(T.LX, SLX, far, mask_far, 0, 4, S.arrAX)
    g.wait_ge(S.stx0, 1)
    g.wait_ge(S.stx1, 2)
    sent += send(T.LX, SLX, far, mask_far, 4, 8, S.arrAX)
    sent += send(T.LX, SLX, near, mask_side, 0, SLX, S.arrCX)
    g.wait_ge(S.sty0, 2)
    sent += send(T.LY0, SLY, far, mask_far, 0, SLY, S.arrAY0)
    g.wait_ge(S.sty1, 2)
    sent += send(T.LY1, SLY, far, mask_far, 0, SLY, S.arrAY1)
    g.wait_ge(S.arrAX, n_ax)
    sent += send(T.LX, SLX, near, mask_near, SLX, grp * SLX, S.arrCX)
    g.wait_ge(S.arrAY0, n_ay)
    sent += send(T.LY0, SLY, near, mask_near, 0, grp * SLY, S.arrCY0)
    g.wait_ge(S.arrAY1, n_ay)
    sent += send(T.LY1, SLY, near, mask_near, 0, grp * SLY, S.arrCY1)
    g.wait_ge(S.sent, sent)

    fN = float(N)

    def names(h):
        k = str(h)
        sc = T["sc" + k]
        return dict(k=k, px=T["px" + k], py=T["py" + k], LY=T["LY" + k], d=T["W" + k], W2=T["W2" + k],
                    sa=T["sa" + k], sb=T["sb" + k], jb=T["jb" + k], ja=T["ja" + k],
                    Mv=T.LX[:, 4 * h:N * SLX:SLX], Qv=T.LX[:, QCOL[h]:N * SLX:SLX],
                    Yv=T["LY" + k][:, 0:N * SLY:SLY], Pv=T["LY" + k][:, 1:N * SLY:SLY],
                    nsm=sc[:, 0:1], nsy=sc[:, 1:2], rc=sc[:, 2:3],
                    den=T["sa" + k][:, N - 1:N], cv=T["sb" + k][:, N - 1:N])

    def x_landed(q):
        for nm, n in (("stm0", 1), ("stx0", 1), ("stx1", 2), ("arrAX", n_ax), ("arrCX", n_cx)):
            q.wait_ge(S[nm], n)

    def y_landed(q, k):
        for nm, n in (("sty" + k, 2), ("arrAY" + k, n_ay), ("arrCY" + k, n_c)):
            q.wait_ge(S[nm], n)

    def v_nsm(h):
        c = names(h)
        x_landed(dve)
        dve.tensor_reduce(c["nsm"], c["Mv"], X, A.add, negate=True).then_inc(S["nsm" + c["k"]], 1)

    def v_d(h):
        c = names(h)
        dve.wait_ge(S["nsm" + c["k"]], 1)
        dve.tensor_scalar(c["d"][:], c["Mv"], fN, c["nsm"], A.mult, A.add).then_inc(S["d" + c["k"]], 1)

    def v_den(h):
        c = names(h)
        dve.wait_ge(S["dd" + c["k"]], 1)
        dve.tensor_tensor_scan(c["sa"][:], c["Qv"], c["jb"][:], fN * EPS, A.add, A.add).then_inc(S["den" + c["k"]], 1)

    def v_rc(h):
        c = names(h)
        dve.wait_ge(S["den" + c["k"]], 1)
        dve.reciprocal(c["rc"], c["den"]).then_inc(S["rc" + c["k"]], 1)

    def v_de(h):
        c = names(h)
        y_landed(dve, c["k"])
        dve.wait_ge(S["d" + c["k"]], 1)
        dve.tensor_tensor(c["W2"][:], c["d"][:], c["Yv"], A.mult).then_inc(S["de" + c["k"]], 1)

    def v_cv(h):
        c = names(h)
        dve.wait_ge(S["de" + c["k"]], 1)
        dve.tensor_tensor_scan(c["sb"][:], c["Pv"], c["W2"][:], 0.0, A.add, A.add).then_inc(S["cv" + c["k"]], 1)

    def v_u(h):
        c = names(h)
        for nm in ("cv", "rc", "xd"):
            dve.wait_ge(S[nm + c["k"]], 1)
        dve.tensor_scalar(T["u" + c["k"]][:], c["px"][:, 0:HB], c["rc"], c["cv"], A.mult, A.mult).then_inc(S["u" + c["k"]], 1)

    def v_v(h):
        c = names(h)
        dve.wait_ge(S["u" + c["k"]], 1)
        dve.wait_ge(S["dye" + c["k"]], 1)
        dve.tensor_tensor(T["v" + c["k"]][:], c["py"][:, 0:HB], T["u" + c["k"]][:], A.subtract).then_inc(S["v" + c["k"]], 1)

    def s_dd(h):
        c = names(h)
        x_landed(act)
        act.wait_ge(S["nsm" + c["k"]], 1)
        act.activation(c["jb"][:], c["Mv"], F.Square, bias=c["nsm"], scale=fN).then_inc(S["dd" + c["k"]], 1)

    def s_xd(h):
        c = names(h)
        act.wait_ge(S["d" + c["k"]], 1)
        act.wait_ge(S["xs" + c["k"]], 1)
        act.activation(c["px"][:, 0:HB], c["px"][:, 0:HB], F.Identity, bias=c["d"][:, 0:1]).then_inc(S["xd" + c["k"]], 1)

    def s_nsy(h):
        c = names(h)
        y_landed(act, c["k"])
        act.activation(c["ja"][:], c["Yv"], F.Copy, scale=-1.0 / fN, accum_out=c["nsy"]).then_inc(S["nsy" + c["k"]], 1)

    def s_dye(h):
        c = names(h)
        act.wait_ge(S["nsy" + c["k"]], 1)
        act.wait_ge(S["e" + c["k"]], 1)
        act.activation(c["py"][:, 0:HB], c["py"][:, 0:HB], F.Identity, bias=c["nsy"]).then_inc(S["dye" + c["k"]], 1)

    def s_diag(h):
        c = names(h)
        act.wait_ge(S["rc" + c["k"]], 1)
        act.wait_ge(S.idN, 1)
        act.activation(T["diag" + c["k"]][:], T.identN[:], F.Sqrt, scale=c["rc"]).then_inc(S["diag" + c["k"]], 1)

    for f, h in ((v_nsm, 0), (v_nsm, 1), (v_d, 0), (v_d, 1), (v_den, 0), (v_den, 1), (v_de, 0), (v_rc, 0), (v_cv, 0),
                 (v_rc, 1), (v_de, 1), (v_u, 0), (v_cv, 1), (v_v, 0), (v_u, 1), (v_v, 1)):
        f(h)
    for f, h in ((s_dd, 0), (s_dd, 1), (s_xd, 0), (s_xd, 1), (s_nsy, 0), (s_dye, 0), (s_nsy, 1), (s_diag, 0),
                 (s_dye, 1), (s_diag, 1)):
        f(h)

    pe.wait_ge(S.v0, 1)
    pe.wait_ge(S.diag0, 1)
    pe.matmul(T.po0[:, 0:HB], T.v0[:], T.diag0[:], True, True).then_inc(S.po0, 1)
    pe.wait_ge(S.v1, 1)
    pe.wait_ge(S.diag1, 1)
    pe.matmul(T.po1[:, 0:HQ], T.v1[:], T.diag1[:, 0:HQ], True, True).then_inc(S.po1, 1)
    pe.matmul(T.pq[:, 0:HQ], T.v1[:], T.diag1[:, HQ:HB], True, True).then_inc(S.pq, 1)

    act.wait_ge(S.po0, 1)
    act.activation(T.ob0[:], T.po0[:, 0:HB], F.Copy).then_inc(S.ob0, 1)
    sp.wait_ge(S.ob0, 1)
    sp.dma_start(T.dx[:, 0:HB], T.ob0[:]).then_inc(S.store0, 16)
    act.wait_ge(S.po1, 1)
    act.activation(T.ob1[:, 0:HQ], T.po1[:, 0:HQ], F.Copy).then_inc(S.ob1, 1)
    dve.wait_ge(S.pq, 1)
    dve.tensor_copy(T.ob1[:, HQ:HB], T.pq[:, 0:HQ]).then_inc(S.ob1, 1)
    sp.wait_ge(S.ob1, 2)
    sp.dma_start(T.dx[:, HB:2 * HB], T.ob1[:]).then_inc(S.store1, 16)
    for h in (0, 1):
        sp.wait_ge(S["store%d" % h], 16)
